import numpy as np
CORES = [56,61,80,85]
N = 4
F = 32
TK = N * F
EPS = 0.01
def setup_inputs(rng):
    return {"x": rng.standard_normal((N, 128, TK), dtype=np.float32) * (0.5 + np.abs(rng.standard_normal((1, 1, TK), dtype=np.float32)))}
def setup_inputs_big(rng):
    d = setup_inputs(rng)
    for k in ("x",): d[k] = (d[k].astype(np.float32) * 1024.0).astype(d[k].dtype)
    return d
def setup_inputs_small(rng):
    d = setup_inputs(rng)
    for k in ("x",): d[k] = (d[k].astype(np.float32) * (1 / 1024.0)).astype(d[k].dtype)
    return d
def setup_inputs_apart(rng):
    d = setup_inputs(rng)
    f = (10.0 ** rng.permutation(np.linspace(-1.5, 1.5, N))).astype(np.float32).reshape(N, 1, 1)
    for k in ("x",): d[k] = (d[k].astype(np.float32) * f).astype(d[k].dtype)
    return d
def setup_inputs_mixed(rng):
    d = setup_inputs(rng)
    f = (10.0 ** rng.uniform(-3, 3, (1, 1, TK))).astype(np.float32); shape = rng.integers(2, size=(1, 1, TK))
    for k in ("x",):
        x = d[k].astype(np.float32)
        other = x * np.where(rng.random((1, 128, TK)) < 0.5, 0.1, 1.0).astype(np.float32)
        d[k] = (np.where(shape == 1, other, x) * f).astype(d[k].dtype)
    return d
def reference(x):
    s = x.astype(np.float64).sum(axis=0)
    n = s / np.sqrt((s ** 2).sum(axis=0) / 128 + EPS)
    return {"y": np.stack([n[:, F * r:F * r + F] for r in range(N)]).astype(np.float32)}

@@ -1,0 +1,156 @@
+from concourse.bass import DstId, RemoteDMATransfer
+from concourse.mybir import AluOpType, ActivationFunctionType
+
+SIM_CORES = 96
+F = 32
+P = 128
+EPS = 0.01
+GA = 2.0 ** -44
+GB = 2.0 ** -22
+E_HOP1 = 4
+E_HOP2 = 8
+
+SCRATCH = {
+    "far": ("dram", [2, P, F], "float32"),
+    "hin": ("dram", [2, P, F], "float32"),
+    "xs": ("sbuf", [P, 2 * F], "float32"),
+    "peer": ("sbuf", [P, F], "float32"),
+    "rem": ("sbuf", [P, F], "float32"),
+    "wa": ("sbuf", [P, P], "float32"),
+    "wb": ("sbuf", [P, P], "float32"),
+    "a": ("sbuf", [P, F], "float32"),
+    "s": ("sbuf", [P, F], "float32"),
+    "sq": ("sbuf", [P, F], "float32"),
+    "q": ("sbuf", [P, F], "float32"),
+    "tb": ("sbuf", [P, F], "float32"),
+    "rm": ("sbuf", [P, F], "float32"),
+    "t": ("sbuf", [P, F], "float32"),
+    "yo": ("sbuf", [P, F], "float32"),
+    "psa": ("psum", [P, 512], "float32"),
+    "psb": ("psum", [P, 512], "float32"),
+}
+SEMAPHORES = ["ld_far", "ld_near", "cst", "sent", "hgot", "got_peer", "got_rem", "s_a", "s_s", "s_sq", "s_mma",
+              "s_mmb", "s_q", "s_tb", "s_rm", "s_t", "s_y", "st"]
+
+
+def _engines(mask):
+    return [e for e in range(mask.bit_length()) if (mask >> e) & 1]
+
+
+def _mask_of(engines):
+    m = 0
+    for e in engines:
+        m |= 1 << e
+    return m
+
+
+def _dst(topo, c):
+    rid, pid, _ = topo.addr(c)
+    return DstId(rid=rid, pnc=pid)
+
+
+def _relays(cores, topo):
+    relay, used = {}, set(cores)
+    for ch in sorted(set(topo.chip(c) for c in cores)):
+        for d in cores:
+            if topo.chip(d) == ch:
+                continue
+            can = [k for k in range(SIM_CORES) if topo.chip(k) == ch and k not in used and topo.may_write(k, d)]
+            same_die = [k for k in can if topo.die(k) == topo.die(d)]
+            relay[(ch, d)] = (same_die or can)[0]
+            used.add(relay[(ch, d)])
+    return relay
+
+
+def _relay_program(g, core, T, topo, cores, dest):
+    n_src = len([c for c in cores if topo.chip(c) == topo.chip(core)])
+    eng = _engines(topo.mask(core, dest))[:E_HOP2]
+    g.wait_ge(T.sem.hgot, E_HOP1 * n_src)
+    g.remote_dma_fused([RemoteDMATransfer(dst_ids=[_dst(topo, dest)], dma_engine_mask=_mask_of(eng),
+                                          remote_sem=T.sem.got_rem, srcs=[T.hin[k] for k in range(n_src)],
+                                          dsts=[T.rem[:]], alu_op=1)], local_sem=T.sem.sent)
+    g.wait_ge(T.sem.sent, len(eng))
+
+
+def rank_program(g, core, T, topo):
+    cores = [int(c) for c in T.cores]
+    relay = _relays(cores, topo)
+    rank = T.rank_of(core)
+    if rank is None:
+        for (ch, d), k in relay.items():
+            if k == core:
+                _relay_program(g, core, T, topo, cores, d)
+        return
+
+    sem = T.sem
+    here = topo.chip(core)
+    near = [c for c in cores if topo.chip(c) == here]
+    far = [c for c in cores if topo.chip(c) != here]
+    slot = near.index(core)
+    lo = F * cores.index(near[0])
+
+    queues = [g.sync, g.scalar]
+    for k, d in enumerate(far):
+        c0 = F * cores.index(d)
+        queues[k % 2].dma_start(T.far[k], T.x[:, c0:c0 + F]).then_inc(sem.ld_far, 16)
+    g.sync.dma_start(T.xs[:], T.x[:, lo:lo + F * len(near)]).then_inc(sem.ld_near, 16)
+
+    g.vector.memset(T.wa[:], GA / P).then_inc(sem.cst, 1)
+    g.vector.memset(T.wb[:], GB / P).then_inc(sem.cst, 1)
+
+    common = topo.mask(core, relay[(here, far[0])])
+    for d in far:
+        common &= topo.mask(core, relay[(here, d)])
+    pool = _engines(common)
+    sets = [pool[k::len(far)][:E_HOP1] for k in range(len(far))]
+    g.wait_ge(sem.ld_far, 16 * len(far))
+    g.remote_dma_fused([RemoteDMATransfer(dst_ids=[_dst(topo, relay[(here, d)])], dma_engine_mask=_mask_of(sets[k]),
+                                          remote_sem=sem.hgot, src=T.far[k], dst=T.hin[slot])
+                        for k, d in enumerate(far)], local_sem=sem.sent)
+    n_sent = E_HOP1 * len(far)
+    peer_eng = sorted(e for s_ in sets for e in s_)
+    for p in near:
+        if p == core:
+            continue
+        rid, pid, _ = topo.addr(p)
+        j = F * near.index(p)
+        g.wait_ge(sem.ld_near, 16)
+        g.remote_dma(T.peer[:], T.xs[:, j:j + F], sem.got_peer, sem.sent, pid, rid,
+                     _mask_of(peer_eng) & topo.mask(core, p))
+        n_sent += len(peer_eng)
+
+    v, sc, te = g.vector, g.scalar, g.tensor
+    j = F * slot
+    v.wait_ge(sem.ld_near, 16)
+    v.wait_ge(sem.got_peer, len(peer_eng))
+    v.tensor_tensor(T.a[:], T.xs[:, j:j + F], T.peer[:], AluOpType.add).then_inc(sem.s_a, 1)
+    v.wait_ge(sem.s_a, 1)
+    v.wait_ge(sem.got_rem, E_HOP2)
+    v.tensor_tensor(T.s[:], T.a[:], T.rem[:], AluOpType.add).then_inc(sem.s_s, 1)
+
+    sc.wait_ge(sem.s_s, 1)
+    sc.activation(T.sq[:], T.s[:], ActivationFunctionType.Square).then_inc(sem.s_sq, 1)
+
+    te.wait_ge(sem.cst, 2)
+    te.wait_ge(sem.s_sq, 1)
+    te.matmul(T.psa[:, 0:F], T.wa[:], T.sq[:], True, True).then_inc(sem.s_mma, 1)
+    te.matmul(T.psb[:, 0:F], T.wb[:], T.sq[:], True, True).then_inc(sem.s_mmb, 1)
+
+    sc.wait_ge(sem.s_mma, 1)
+    sc.activation(T.q[:], T.psa[:, 0:F], ActivationFunctionType.Sqrt, bias=GA * EPS).then_inc(sem.s_q, 1)
+
+    v.wait_ge(sem.s_s, 1)
+    v.wait_ge(sem.s_mmb, 1)
+    v.tensor_scalar(T.tb[:], T.psb[:, 0:F], GB * EPS, None, AluOpType.add).then_inc(sem.s_tb, 1)
+    v.wait_ge(sem.s_tb, 1)
+    v.reciprocal(T.rm[:], T.tb[:]).then_inc(sem.s_rm, 1)
+    v.wait_ge(sem.s_rm, 1)
+    v.tensor_tensor(T.t[:], T.s[:], T.rm[:], AluOpType.mult).then_inc(sem.s_t, 1)
+    v.wait_ge(sem.s_t, 1)
+    v.wait_ge(sem.s_q, 1)
+    v.tensor_tensor(T.yo[:], T.t[:], T.q[:], AluOpType.mult).then_inc(sem.s_y, 1)
+
+    g.sync.wait_ge(sem.s_y, 1)
+    g.sync.dma_start(T.y[:], T.yo[:]).then_inc(sem.st, 16)
+    g.sync.wait_ge(sem.st, 16)
+    g.wait_ge(sem.sent, n_sent)

@@ -18,11 +18,12 @@ SCRATCH = {
     "rem": ("sbuf", [P, F], "float32"),
     "wa": ("sbuf", [P, P], "float32"),
     "wb": ("sbuf", [P, P], "float32"),
+    "e2": ("sbuf", [P, F], "float32"),
+    "ev": ("sbuf", [P, F], "float32"),
     "a": ("sbuf", [P, F], "float32"),
     "s": ("sbuf", [P, F], "float32"),
     "sq": ("sbuf", [P, F], "float32"),
     "q": ("sbuf", [P, F], "float32"),
-    "tb": ("sbuf", [P, F], "float32"),
     "rm": ("sbuf", [P, F], "float32"),
     "t": ("sbuf", [P, F], "float32"),
     "yo": ("sbuf", [P, F], "float32"),
@@ -30,7 +31,7 @@ SCRATCH = {
     "psb": ("psum", [P, 512], "float32"),
 }
 SEMAPHORES = ["ld_far", "ld_near", "cst", "sent", "hgot", "got_peer", "got_rem", "s_a", "s_s", "s_sq", "s_mma",
-              "s_mmb", "s_q", "s_tb", "s_rm", "s_t", "s_y", "st"]
+              "s_mmb", "s_q", "c_e2", "s_ev", "s_rm", "s_t", "s_y", "st"]
 
 
 def _engines(mask):
@@ -83,6 +84,7 @@ def rank_program(g, core, T, topo):
         return
 
     sem = T.sem
+    v, sc, te = g.vector, g.scalar, g.tensor
     here = topo.chip(core)
     near = [c for c in cores if topo.chip(c) == here]
     far = [c for c in cores if topo.chip(c) != here]
@@ -95,8 +97,14 @@ def rank_program(g, core, T, topo):
         queues[k % 2].dma_start(T.far[k], T.x[:, c0:c0 + F]).then_inc(sem.ld_far, 16)
     g.sync.dma_start(T.xs[:], T.x[:, lo:lo + F * len(near)]).then_inc(sem.ld_near, 16)
 
-    g.vector.memset(T.wa[:], GA / P).then_inc(sem.cst, 1)
-    g.vector.memset(T.wb[:], GB / P).then_inc(sem.cst, 1)
+    v.memset(T.e2[:], EPS * EPS).then_inc(sem.c_e2, 1)
+    v.memset(T.wb[:], GB / P).then_inc(sem.cst, 1)
+    v.memset(T.wa[:], GA / P).then_inc(sem.cst, 1)
+    sc.wait_ge(sem.c_e2, 1)
+    sc.activation(T.ev[:], T.e2[:], ActivationFunctionType.Sqrt).then_inc(sem.s_ev, 1)
+    te.wait_ge(sem.cst, 2)
+    te.wait_ge(sem.s_ev, 1)
+    te.matmul(T.psb[:, 0:F], T.wb[:], T.ev[:], True, False)
 
     common = topo.mask(core, relay[(here, far[0])])
     for d in far:
@@ -119,7 +127,6 @@ def rank_program(g, core, T, topo):
                      _mask_of(peer_eng) & topo.mask(core, p))
         n_sent += len(peer_eng)
 
-    v, sc, te = g.vector, g.scalar, g.tensor
     j = F * slot
     v.wait_ge(sem.ld_near, 16)
     v.wait_ge(sem.got_peer, len(peer_eng))
@@ -131,19 +138,16 @@ def rank_program(g, core, T, topo):
     sc.wait_ge(sem.s_s, 1)
     sc.activation(T.sq[:], T.s[:], ActivationFunctionType.Square).then_inc(sem.s_sq, 1)
 
-    te.wait_ge(sem.cst, 2)
     te.wait_ge(sem.s_sq, 1)
+    te.matmul(T.psb[:, 0:F], T.wb[:], T.sq[:], False, True).then_inc(sem.s_mmb, 1)
     te.matmul(T.psa[:, 0:F], T.wa[:], T.sq[:], True, True).then_inc(sem.s_mma, 1)
-    te.matmul(T.psb[:, 0:F], T.wb[:], T.sq[:], True, True).then_inc(sem.s_mmb, 1)
 
     sc.wait_ge(sem.s_mma, 1)
     sc.activation(T.q[:], T.psa[:, 0:F], ActivationFunctionType.Sqrt, bias=GA * EPS).then_inc(sem.s_q, 1)
 
     v.wait_ge(sem.s_s, 1)
     v.wait_ge(sem.s_mmb, 1)
-    v.tensor_scalar(T.tb[:], T.psb[:, 0:F], GB * EPS, None, AluOpType.add).then_inc(sem.s_tb, 1)
-    v.wait_ge(sem.s_tb, 1)
-    v.reciprocal(T.rm[:], T.tb[:]).then_inc(sem.s_rm, 1)
+    v.reciprocal(T.rm[:], T.psb[:, 0:F]).then_inc(sem.s_rm, 1)
     v.wait_ge(sem.s_rm, 1)
     v.tensor_tensor(T.t[:], T.s[:], T.rm[:], AluOpType.mult).then_inc(sem.s_t, 1)
     v.wait_ge(sem.s_t, 1)

@@ -6,14 +6,20 @@ F = 32
 P = 128
 EPS = 0.01
 GA = 2.0 ** -44
-GB = 2.0 ** -22
-E_HOP1 = 4
+GS = 2.0 ** 22
+E_HOP1 = 2
+E_PEER = 4
+HEAD = 8
 E_HOP2 = 8
 
 SCRATCH = {
     "far": ("dram", [2, P, F], "float32"),
     "hin": ("dram", [2, P, F], "float32"),
-    "xs": ("sbuf", [P, 2 * F], "float32"),
+    "pa_s": ("dram", [P, HEAD * F // P], "float32"),
+    "pb_s": ("dram", [P, (P - HEAD) * F // P], "float32"),
+    "pa_r": ("dram", [P, HEAD * F // P], "float32"),
+    "pb_r": ("dram", [P, (P - HEAD) * F // P], "float32"),
+    "xo": ("sbuf", [P, F], "float32"),
     "peer": ("sbuf", [P, F], "float32"),
     "rem": ("sbuf", [P, F], "float32"),
     "wa": ("sbuf", [P, P], "float32"),
@@ -25,13 +31,14 @@ SCRATCH = {
     "sq": ("sbuf", [P, F], "float32"),
     "q": ("sbuf", [P, F], "float32"),
     "rm": ("sbuf", [P, F], "float32"),
+    "s2": ("sbuf", [P, F], "float32"),
     "t": ("sbuf", [P, F], "float32"),
     "yo": ("sbuf", [P, F], "float32"),
     "psa": ("psum", [P, 512], "float32"),
     "psb": ("psum", [P, 512], "float32"),
 }
-SEMAPHORES = ["ld_far", "ld_near", "cst", "sent", "hgot", "got_peer", "got_rem", "s_a", "s_s", "s_sq", "s_mma",
-              "s_mmb", "s_q", "c_e2", "s_ev", "s_rm", "s_t", "s_y", "st"]
+SEMAPHORES = ["ld_far", "ld_pa", "ld_pb", "ld_own", "ld_p", "got_pa", "got_pb", "cst", "sent", "hgot", "got_rem",
+              "s_a", "s_s", "s_sq", "s_mma", "s_mmb", "s_q", "c_e2", "s_ev", "s_rm", "s_s2", "s_t", "s_y", "st"]
 
 
 def _engines(mask):
@@ -89,16 +96,24 @@ def rank_program(g, core, T, topo):
     near = [c for c in cores if topo.chip(c) == here]
     far = [c for c in cores if topo.chip(c) != here]
     slot = near.index(core)
-    lo = F * cores.index(near[0])
+    nb = [c for c in near if c != core][0]
 
-    queues = [g.sync, g.scalar]
+    c0 = F * cores.index(nb)
+    g.sync.dma_start(T.pa_s[:], T.x[0:HEAD, c0:c0 + F]).then_inc(sem.ld_pa, 16)
+    queues = [g.scalar, g.sync]
     for k, d in enumerate(far):
-        c0 = F * cores.index(d)
-        queues[k % 2].dma_start(T.far[k], T.x[:, c0:c0 + F]).then_inc(sem.ld_far, 16)
-    g.sync.dma_start(T.xs[:], T.x[:, lo:lo + F * len(near)]).then_inc(sem.ld_near, 16)
+        c1 = F * cores.index(d)
+        queues[k % 2].dma_start(T.far[k], T.x[:, c1:c1 + F]).then_inc(sem.ld_far, 16)
+    g.scalar.dma_start(T.pb_s[:], T.x[HEAD:P, c0:c0 + F]).then_inc(sem.ld_pb, 16)
+    c0 = F * rank
+    g.sync.dma_start(T.xo[:], T.x[:, c0:c0 + F]).then_inc(sem.ld_own, 16)
+    g.sync.wait_ge(sem.got_pa, E_HOP1 * len(far))
+    g.sync.dma_start(T.peer[0:HEAD, :], T.pa_r[:]).then_inc(sem.ld_p, 16)
+    g.sync.wait_ge(sem.got_pb, E_PEER)
+    g.sync.dma_start(T.peer[HEAD:P, :], T.pb_r[:]).then_inc(sem.ld_p, 16)
 
     v.memset(T.e2[:], EPS * EPS).then_inc(sem.c_e2, 1)
-    v.memset(T.wb[:], GB / P).then_inc(sem.cst, 1)
+    v.memset(T.wb[:], 1.0 / P).then_inc(sem.cst, 1)
     v.memset(T.wa[:], GA / P).then_inc(sem.cst, 1)
     sc.wait_ge(sem.c_e2, 1)
     sc.activation(T.ev[:], T.e2[:], ActivationFunctionType.Sqrt).then_inc(sem.s_ev, 1)
@@ -106,31 +121,28 @@ def rank_program(g, core, T, topo):
     te.wait_ge(sem.s_ev, 1)
     te.matmul(T.psb[:, 0:F], T.wb[:], T.ev[:], True, False)
 
-    common = topo.mask(core, relay[(here, far[0])])
+    common = topo.mask(core, nb)
     for d in far:
         common &= topo.mask(core, relay[(here, d)])
     pool = _engines(common)
-    sets = [pool[k::len(far)][:E_HOP1] for k in range(len(far))]
+    step = len(pool) // (E_HOP1 * len(far))
+    spread = pool[::step]
+    sets = [spread[k::len(far)][:E_HOP1] for k in range(len(far))]
+    peer_eng = pool[step // 2::step][:E_PEER]
+    rid, pid, _ = topo.addr(nb)
+    g.wait_ge(sem.ld_pa, 16)
+    g.remote_dma(T.pa_r[:], T.pa_s[:], sem.got_pa, sem.sent, pid, rid, _mask_of(spread[:E_HOP1 * len(far)]))
     g.wait_ge(sem.ld_far, 16 * len(far))
     g.remote_dma_fused([RemoteDMATransfer(dst_ids=[_dst(topo, relay[(here, d)])], dma_engine_mask=_mask_of(sets[k]),
                                           remote_sem=sem.hgot, src=T.far[k], dst=T.hin[slot])
                         for k, d in enumerate(far)], local_sem=sem.sent)
-    n_sent = E_HOP1 * len(far)
-    peer_eng = sorted(e for s_ in sets for e in s_)
-    for p in near:
-        if p == core:
-            continue
-        rid, pid, _ = topo.addr(p)
-        j = F * near.index(p)
-        g.wait_ge(sem.ld_near, 16)
-        g.remote_dma(T.peer[:], T.xs[:, j:j + F], sem.got_peer, sem.sent, pid, rid,
-                     _mask_of(peer_eng) & topo.mask(core, p))
-        n_sent += len(peer_eng)
+    g.wait_ge(sem.ld_pb, 16)
+    g.remote_dma(T.pb_r[:], T.pb_s[:], sem.got_pb, sem.sent, pid, rid, _mask_of(peer_eng))
+    n_sent = 2 * E_HOP1 * len(far) + len(peer_eng)
 
-    j = F * slot
-    v.wait_ge(sem.ld_near, 16)
-    v.wait_ge(sem.got_peer, len(peer_eng))
-    v.tensor_tensor(T.a[:], T.xs[:, j:j + F], T.peer[:], AluOpType.add).then_inc(sem.s_a, 1)
+    v.wait_ge(sem.ld_own, 16)
+    v.wait_ge(sem.ld_p, 32)
+    v.tensor_tensor(T.a[:], T.xo[:], T.peer[:], AluOpType.add).then_inc(sem.s_a, 1)
     v.wait_ge(sem.s_a, 1)
     v.wait_ge(sem.got_rem, E_HOP2)
     v.tensor_tensor(T.s[:], T.a[:], T.rem[:], AluOpType.add).then_inc(sem.s_s, 1)
@@ -146,13 +158,15 @@ def rank_program(g, core, T, topo):
     sc.activation(T.q[:], T.psa[:, 0:F], ActivationFunctionType.Sqrt, bias=GA * EPS).then_inc(sem.s_q, 1)
 
     v.wait_ge(sem.s_s, 1)
+    v.tensor_scalar(T.s2[:], T.s[:], GS, None, AluOpType.mult).then_inc(sem.s_s2, 1)
+    v.wait_ge(sem.s_s2, 1)
     v.wait_ge(sem.s_mmb, 1)
     v.reciprocal(T.rm[:], T.psb[:, 0:F]).then_inc(sem.s_rm, 1)
-    v.wait_ge(sem.s_rm, 1)
-    v.tensor_tensor(T.t[:], T.s[:], T.rm[:], AluOpType.mult).then_inc(sem.s_t, 1)
-    v.wait_ge(sem.s_t, 1)
     v.wait_ge(sem.s_q, 1)
-    v.tensor_tensor(T.yo[:], T.t[:], T.q[:], AluOpType.mult).then_inc(sem.s_y, 1)
+    v.tensor_tensor(T.t[:], T.s2[:], T.q[:], AluOpType.mult).then_inc(sem.s_t, 1)
+    v.wait_ge(sem.s_rm, 1)
+    v.wait_ge(sem.s_t, 1)
+    v.tensor_tensor(T.yo[:], T.t[:], T.rm[:], AluOpType.mult).then_inc(sem.s_y, 1)
 
     g.sync.wait_ge(sem.s_y, 1)
     g.sync.dma_start(T.y[:], T.yo[:]).then_inc(sem.st, 16)

from concourse.bass import DstId, RemoteDMATransfer
from concourse.mybir import AluOpType, ActivationFunctionType

SIM_CORES = 96
F = 32
P = 128
EPS = 0.01
GA = 2.0 ** -44
GS = 2.0 ** 22
E_HOP1 = 2
E_PEER = 4
HEAD = 8
E_HOP2 = 8

SCRATCH = {
    "far": ("dram", [2, P, F], "float32"),
    "hin": ("dram", [2, P, F], "float32"),
    "pa_s": ("dram", [P, HEAD * F // P], "float32"),
    "pb_s": ("dram", [P, (P - HEAD) * F // P], "float32"),
    "pa_r": ("dram", [P, HEAD * F // P], "float32"),
    "pb_r": ("dram", [P, (P - HEAD) * F // P], "float32"),
    "xo": ("sbuf", [P, F], "float32"),
    "peer": ("sbuf", [P, F], "float32"),
    "rem": ("sbuf", [P, F], "float32"),
    "wa": ("sbuf", [P, P], "float32"),
    "wb": ("sbuf", [P, P], "float32"),
    "e2": ("sbuf", [P, F], "float32"),
    "ev": ("sbuf", [P, F], "float32"),
    "a": ("sbuf", [P, F], "float32"),
    "s": ("sbuf", [P, F], "float32"),
    "sq": ("sbuf", [P, F], "float32"),
    "q": ("sbuf", [P, F], "float32"),
    "rm": ("sbuf", [P, F], "float32"),
    "s2": ("sbuf", [P, F], "float32"),
    "t": ("sbuf", [P, F], "float32"),
    "yo": ("sbuf", [P, F], "float32"),
    "psa": ("psum", [P, 512], "float32"),
    "psb": ("psum", [P, 512], "float32"),
}
SEMAPHORES = ["ld_far", "ld_pa", "ld_pb", "ld_own", "ld_p", "got_pa", "got_pb", "cst", "sent", "hgot", "got_rem",
              "s_a", "s_s", "s_sq", "s_mma", "s_mmb", "s_q", "c_e2", "s_ev", "s_rm", "s_s2", "s_t", "s_y", "st"]


def _engines(mask):
    return [e for e in range(mask.bit_length()) if (mask >> e) & 1]


def _mask_of(engines):
    m = 0
    for e in engines:
        m |= 1 << e
    return m


def _dst(topo, c):
    rid, pid, _ = topo.addr(c)
    return DstId(rid=rid, pnc=pid)


def _relays(cores, topo):
    relay, used = {}, set(cores)
    for ch in sorted(set(topo.chip(c) for c in cores)):
        for d in cores:
            if topo.chip(d) == ch:
                continue
            can = [k for k in range(SIM_CORES) if topo.chip(k) == ch and k not in used and topo.may_write(k, d)]
            same_die = [k for k in can if topo.die(k) == topo.die(d)]
            relay[(ch, d)] = (same_die or can)[0]
            used.add(relay[(ch, d)])
    return relay


def _relay_program(g, core, T, topo, cores, dest):
    n_src = len([c for c in cores if topo.chip(c) == topo.chip(core)])
    eng = _engines(topo.mask(core, dest))[:E_HOP2]
    g.wait_ge(T.sem.hgot, E_HOP1 * n_src)
    g.remote_dma_fused([RemoteDMATransfer(dst_ids=[_dst(topo, dest)], dma_engine_mask=_mask_of(eng),
                                          remote_sem=T.sem.got_rem, srcs=[T.hin[k] for k in range(n_src)],
                                          dsts=[T.rem[:]], alu_op=1)], local_sem=T.sem.sent)
    g.wait_ge(T.sem.sent, len(eng))


def rank_program(g, core, T, topo):
    cores = [int(c) for c in T.cores]
    relay = _relays(cores, topo)
    rank = T.rank_of(core)
    if rank is None:
        for (ch, d), k in relay.items():
            if k == core:
                _relay_program(g, core, T, topo, cores, d)
        return

    sem = T.sem
    v, sc, te = g.vector, g.scalar, g.tensor
    here = topo.chip(core)
    near = [c for c in cores if topo.chip(c) == here]
    far = [c for c in cores if topo.chip(c) != here]
    slot = near.index(core)
    nb = [c for c in near if c != core][0]

    c0 = F * cores.index(nb)
    g.sync.dma_start(T.pa_s[:], T.x[0:HEAD, c0:c0 + F]).then_inc(sem.ld_pa, 16)
    queues = [g.scalar, g.sync]
    for k, d in enumerate(far):
        c1 = F * cores.index(d)
        queues[k % 2].dma_start(T.far[k], T.x[:, c1:c1 + F]).then_inc(sem.ld_far, 16)
    g.scalar.dma_start(T.pb_s[:], T.x[HEAD:P, c0:c0 + F]).then_inc(sem.ld_pb, 16)
    c0 = F * rank
    g.sync.dma_start(T.xo[:], T.x[:, c0:c0 + F]).then_inc(sem.ld_own, 16)
    g.sync.wait_ge(sem.got_pa, E_HOP1 * len(far))
    g.sync.dma_start(T.peer[0:HEAD, :], T.pa_r[:]).then_inc(sem.ld_p, 16)
    g.sync.wait_ge(sem.got_pb, E_PEER)
    g.sync.dma_start(T.peer[HEAD:P, :], T.pb_r[:]).then_inc(sem.ld_p, 16)

    v.memset(T.e2[:], EPS * EPS).then_inc(sem.c_e2, 1)
    v.memset(T.wb[:], 1.0 / P).then_inc(sem.cst, 1)
    v.memset(T.wa[:], GA / P).then_inc(sem.cst, 1)
    sc.wait_ge(sem.c_e2, 1)
    sc.activation(T.ev[:], T.e2[:], ActivationFunctionType.Sqrt).then_inc(sem.s_ev, 1)
    te.wait_ge(sem.cst, 2)
    te.wait_ge(sem.s_ev, 1)
    te.matmul(T.psb[:, 0:F], T.wb[:], T.ev[:], True, False)

    common = topo.mask(core, nb)
    for d in far:
        common &= topo.mask(core, relay[(here, d)])
    pool = _engines(common)
    step = len(pool) // (E_HOP1 * len(far))
    spread = pool[::step]
    sets = [spread[k::len(far)][:E_HOP1] for k in range(len(far))]
    peer_eng = pool[step // 2::step][:E_PEER]
    rid, pid, _ = topo.addr(nb)
    g.wait_ge(sem.ld_pa, 16)
    g.remote_dma(T.pa_r[:], T.pa_s[:], sem.got_pa, sem.sent, pid, rid, _mask_of(spread[:E_HOP1 * len(far)]))
    g.wait_ge(sem.ld_far, 16 * len(far))
    g.remote_dma_fused([RemoteDMATransfer(dst_ids=[_dst(topo, relay[(here, d)])], dma_engine_mask=_mask_of(sets[k]),
                                          remote_sem=sem.hgot, src=T.far[k], dst=T.hin[slot])
                        for k, d in enumerate(far)], local_sem=sem.sent)
    g.wait_ge(sem.ld_pb, 16)
    g.remote_dma(T.pb_r[:], T.pb_s[:], sem.got_pb, sem.sent, pid, rid, _mask_of(peer_eng))
    n_sent = 2 * E_HOP1 * len(far) + len(peer_eng)

    v.wait_ge(sem.ld_own, 16)
    v.wait_ge(sem.ld_p, 32)
    v.tensor_tensor(T.a[:], T.xo[:], T.peer[:], AluOpType.add).then_inc(sem.s_a, 1)
    v.wait_ge(sem.s_a, 1)
    v.wait_ge(sem.got_rem, E_HOP2)
    v.tensor_tensor(T.s[:], T.a[:], T.rem[:], AluOpType.add).then_inc(sem.s_s, 1)

    sc.wait_ge(sem.s_s, 1)
    sc.activation(T.sq[:], T.s[:], ActivationFunctionType.Square).then_inc(sem.s_sq, 1)

    te.wait_ge(sem.s_sq, 1)
    te.matmul(T.psb[:, 0:F], T.wb[:], T.sq[:], False, True).then_inc(sem.s_mmb, 1)
    te.matmul(T.psa[:, 0:F], T.wa[:], T.sq[:], True, True).then_inc(sem.s_mma, 1)

    sc.wait_ge(sem.s_mma, 1)
    sc.activation(T.q[:], T.psa[:, 0:F], ActivationFunctionType.Sqrt, bias=GA * EPS).then_inc(sem.s_q, 1)

    v.wait_ge(sem.s_s, 1)
    v.tensor_scalar(T.s2[:], T.s[:], GS, None, AluOpType.mult).then_inc(sem.s_s2, 1)
    v.wait_ge(sem.s_s2, 1)
    v.wait_ge(sem.s_mmb, 1)
    v.reciprocal(T.rm[:], T.psb[:, 0:F]).then_inc(sem.s_rm, 1)
    v.wait_ge(sem.s_q, 1)
    v.tensor_tensor(T.t[:], T.s2[:], T.q[:], AluOpType.mult).then_inc(sem.s_t, 1)
    v.wait_ge(sem.s_rm, 1)
    v.wait_ge(sem.s_t, 1)
    v.tensor_tensor(T.yo[:], T.t[:], T.rm[:], AluOpType.mult).then_inc(sem.s_y, 1)

    g.sync.wait_ge(sem.s_y, 1)
    g.sync.dma_start(T.y[:], T.yo[:]).then_inc(sem.st, 16)
    g.sync.wait_ge(sem.st, 16)
    g.wait_ge(sem.sent, n_sent)
